import numpy as np
import ml_dtypes


def mxq(x, axis, fmt="e4m3"):
    dtype, down = {"e4m3": (ml_dtypes.float8_e4m3fn, 7), "e5m2": (ml_dtypes.float8_e5m2, 14)}[fmt]
    v = np.moveaxis(np.asarray(x, np.float32).astype(ml_dtypes.bfloat16).astype(np.float64), axis, -1)
    blocks = v.reshape(v.shape[:-1] + (-1, 32))
    amax = np.abs(blocks).max(-1, keepdims=True)
    byte = np.maximum(np.where(amax > 0, np.frexp(amax)[1] - 1 + 127, 0) - down, 1)
    scale = np.exp2(byte - 127.0)
    codes = (blocks / scale).astype(np.float32).astype(dtype).astype(np.float64)
    return np.moveaxis((codes * scale).reshape(v.shape), -1, axis)


WIDE = False


def mx_kscale(k):
    if not WIDE:
        return np.ones(k)
    levels = np.array([30, -30])
    if k % 512:
        return np.exp2(np.random.permutation(np.resize(levels, k // 32))).repeat(32)
    a = np.empty((k // 512, 16))
    for p in range(k // 512):
        a[p, :8] = np.random.permutation(np.resize(levels, 8))
        for g in range(8):
            far = levels[np.abs(levels - a[p, g]) >= 10]
            a[p, g + 8] = far[np.random.randint(len(far))]
    return np.exp2(a.ravel()).repeat(32)


def f64(x):
    return np.asarray(x).astype(np.float64)


def striped(idx):
    return np.tile(np.asarray(idx).reshape(-1, 16).T, (8, 1)).astype(np.uint16)


def unstriped(offs):
    return offs[:16].T.reshape(-1).astype(np.int64)


def bf(x):
    return np.asarray(x, np.float32).astype(ml_dtypes.bfloat16)


def planes(Y):
    r, m = Y.shape
    b = f64(bf(Y)).reshape(r // 32, 32, m)
    amax = np.abs(b).max(1)
    byte = np.clip(np.where(amax > 0, np.frexp(amax)[1] - 1 + 127 - 7, 1), 1, 254)
    codes = (b * np.exp2(127.0 - byte)[:, None, :]).reshape(r, m).astype(np.float32).astype(ml_dtypes.float8_e4m3fn).view(np.uint8)
    words = codes.reshape(r // 512, 128, 4, m).transpose(0, 1, 3, 2)
    return np.ascontiguousarray(words), np.ascontiguousarray(byte.astype(np.uint8).reshape(r // 512, 16, m))


K, N, T, J = 512, 512, 2048, 512


def setup_inputs():
    n = np.random.standard_normal
    idx = np.random.permutation(T)[:J]
    fj = mx_kscale(J)
    tj = np.ones(T)
    tj[idx] = fj
    return {
        "xt": (n((K, T)) * tj).astype(np.float32),
        "g": (n((N, T)) * np.exp(0.7 * n((1, T))) / tj).astype(np.float32),
        "mom": (1.0 * n((K, N))).astype(np.float32),
        "old": (1.0 * n((K, N))).astype(np.float32),
        "offs": striped(idx),
    }


def reference(xt, g, mom, old, offs):
    idx = unstriped(offs)
    xj = f64(xt)[:, idx].T
    gj = f64(g)[:, idx].T
    xjq = mxq(xj, 0, "e4m3")
    gjq = mxq(gj, 0, "e5m2")
    w = xjq.T @ gjq
    u = 0.04 * w + 0.5 * f64(mom)
    y = 0.3 * f64(old) - u / (np.abs(u) + np.mean(np.abs(u), axis=1, keepdims=True))
    words, scales = planes(y)
    return y, words, scales

@@ -1,0 +1,182 @@
+from contextlib import ExitStack
+
+import concourse.mybir as mybir
+from concourse.masks import make_identity
+
+K, N, T, J = 512, 512, 2048, 512
+FLOPS = 2 * K * N * J
+
+F32 = mybir.dt.float32
+BF16 = mybir.dt.bfloat16
+I32 = mybir.dt.int32
+U32 = mybir.dt.uint32
+U16 = mybir.dt.uint16
+U8 = mybir.dt.uint8
+E4M3 = mybir.dt.float8_e4m3fn_x4
+E5M2 = mybir.dt.float8_e5m2_x4
+ALU = mybir.AluOpType
+ACT = mybir.ActivationFunctionType
+
+P = 128
+PACK = 4
+HALF = N // 2
+
+
+def tile_moe_expert_soft_sign_step_pl_kernel(tc, xt, g, mom, old, offs, out_0, out_1, out_2):
+    nc = tc.nc
+    with ExitStack() as ctx:
+        keep = ctx.enter_context(tc.tile_pool(name="keep", bufs=1))
+        turn_psum = ctx.enter_context(tc.psum_pool(name="turn_psum", bufs=4))
+        sum_psum = ctx.enter_context(tc.psum_pool(name="sum_psum", bufs=1))
+
+        offsets = keep.tile([P, J // 16], U16, name="offsets")
+
+        xt_rows = xt.rearrange("(p t) c -> p t c", t=PACK)
+        mom_rows = mom.rearrange("(p t) n -> p t n", t=PACK)
+        old_rows = old.rearrange("(p t) n -> p t n", t=PACK)
+        y_rows = out_0.rearrange("(p t) n -> p t n", t=PACK)
+
+        g_win = [keep.tile([P, T], F32, name="g_win%d" % b) for b in range(4)]
+        x_win = [keep.tile([P, T], F32, name="x_win%d" % t, tag="x%d" % t, align_bytes=64) for t in range(PACK)]
+        mom_sb = [keep.tile([P, N], F32, name="mom%d" % t) for t in range(PACK)]
+        old_sb = [keep.tile([P, N], F32, name="old%d" % t) for t in range(PACK)]
+
+        nc.sync.dma_start(g_win[0][:], g[0:P, :])
+        nc.sync.dma_start(offsets[:], offs)
+        for b in range(1, 4):
+            nc.sync.dma_start(g_win[b][:], g[b * P : (b + 1) * P, :])
+        for t in range(3):
+            nc.sync.dma_start(x_win[t][:], xt_rows[:, t, :])
+        for t in range(2):
+            nc.sync.dma_start(mom_sb[t][:], mom_rows[:, t, :])
+        nc.sync.dma_start(x_win[3][:], xt_rows[:, 3, :])
+        nc.sync.dma_start(mom_sb[2][:], mom_rows[:, 2, :])
+        nc.sync.dma_start(old_sb[0][:], old_rows[:, 0, :])
+        nc.sync.dma_start(mom_sb[3][:], mom_rows[:, 3, :])
+        for t in (3, 1, 2):
+            nc.sync.dma_start(old_sb[t][:], old_rows[:, t, :])
+
+        warm_in = keep.tile([P, 1], F32, name="warm_in")
+        warm_out = keep.tile([P, 1], F32, name="warm_out")
+        nc.vector.memset(warm_in[:], 1.0)
+        nc.scalar.activation(warm_out[:], warm_in[:], ACT.Abs_reciprocal_sqrt)
+
+        ident = keep.tile([P, P], F32, name="ident")
+        make_identity(nc, ident[:])
+
+        g_grouped = keep.tile([P, N, PACK], BF16, name="g_grouped", align_bytes=64)
+        g_scales = keep.tile([P, N], U8, name="g_scales", align_bytes=64)
+        x_scales = [keep.tile([P, P], U8, name="x_scales%d" % t, align_bytes=64) for t in range(PACK)]
+        w = [sum_psum.tile([P, N], F32, name="w%d" % t) for t in range(PACK)]
+        mag = [keep.tile([P, N], F32, name="mag%d" % t) for t in range(PACK)]
+        mean = [keep.tile([P, 1], F32, name="mean%d" % t) for t in range(PACK)]
+        root = [keep.tile([P, N], F32, name="root%d" % t) for t in range(PACK)]
+        y_grouped = [keep.tile([P, HALF, PACK], BF16, name="y_grouped%d" % h, align_bytes=64) for h in range(2)]
+        y_codes = keep.tile([P, N], U32, name="y_codes", align_bytes=64)
+        y_scales = keep.tile([P, N], U8, name="y_scales", align_bytes=64)
+
+        def gather_and_turn(window, name, grouped):
+            picked = keep.tile([P, J], BF16, name="picked_" + name, tag="picked_" + name)
+            nc.vector.tensor_copy(picked[:], window[:].indirect(offsets[:]))
+            words = picked[:].bitcast(F32)
+            turned = turn_psum.tile([P, 2, P], F32, name="turned")
+            for e in range(2):
+                nc.tensor.transpose(turned[:, e, :], words[:, e::2], ident[:])
+            nc.scalar.copy(grouped.bitcast(F32), turned[:].rearrange("p e r -> p r e"))
+
+        def turn_x(t):
+            grouped = keep.tile([P, P, PACK], BF16, name="x_grouped%d" % t, tag="x_grouped%d" % t, align_bytes=64)
+            gather_and_turn(x_win[t], "x%d" % t, grouped[:])
+            return grouped
+
+        def quantize(grouped, codes, scales, fmt):
+            nc.vector.quantize_mx(out=codes.bitcast(fmt), scales=scales, in_=grouped[:].rearrange("p c t -> p (c t)"))
+
+        def multiply(t, grouped, tag):
+            codes = keep.tile([P, P], U32, name="x_codes%d" % t, tag=tag, align_bytes=64)
+            quantize(grouped, codes[:], x_scales[t][:], E4M3)
+            nc.tensor.matmul_mx(
+                out=w[t][:], lhsT=codes[:].bitcast(E4M3), lhsT_scale=x_scales[t][:],
+                rhs=g_codes[:].bitcast(E5M2), rhs_scale=g_scales[:], start=True, stop=True,
+            )
+
+        def mix(t, u):
+            nc.vector.scalar_tensor_tensor(u, w[t][:], 0.04 / 0.5, mom_sb[t][:], ALU.mult, ALU.add)
+            nc.scalar.activation(mag[t][:], u, ACT.Abs, scale=1.0 / N, accum_out=mean[t][:])
+
+        def inverse_root(t, cols):
+            nc.scalar.activation(root[t][:, cols], mag[t][:, cols], ACT.Abs_reciprocal_sqrt, bias=mean[t][:], scale=float(N))
+
+        def square(t, recip, cols):
+            nc.scalar.activation(recip[:, cols], root[t][:, cols], ACT.Square)
+
+        def soft_sign(u, recip, step, cols):
+            nc.vector.tensor_tensor(step[:, cols], u[:, cols], recip[:, cols], ALU.mult)
+
+        def halves(ap):
+            return ap.rearrange("p (h c) -> p h c", h=2)
+
+        def decay(t, step):
+            nc.vector.scalar_tensor_tensor(y[:, :, t, :], halves(old_sb[t][:]), 0.3, halves(step), ALU.mult, ALU.subtract)
+            nc.sync.dma_start(halves(y_rows[:, t, :]), y[:, :, t, :])
+
+        whole = slice(0, N)
+        half = [slice(h * HALF, (h + 1) * HALF) for h in range(2)]
+        for b in range(4):
+            gather_and_turn(g_win[b], "g%d" % b, g_grouped[:, b * P : (b + 1) * P, :])
+        x0 = turn_x(0)
+        g_codes = keep.tile([P, N], U32, name="g_codes", tag="x0", align_bytes=64)
+        quantize(g_grouped, g_codes[:], g_scales[:], E5M2)
+        x1 = turn_x(1)
+        multiply(0, x0, "x1")
+        x2 = turn_x(2)
+        multiply(1, x1, "x2")
+        u0 = keep.tile([P, N], F32, name="u0")
+        u1 = keep.tile([P, N], F32, name="u1")
+        recip0 = keep.tile([P, N], F32, name="recip0")
+        mix(0, u0[:])
+        inverse_root(0, whole)
+        square(0, recip0, whole)
+        multiply(2, x2, "x_codes2")
+        mix(1, u1[:])
+        inverse_root(1, whole)
+        x3 = turn_x(3)
+        recip1 = keep.tile([P, N], F32, name="recip1", tag="picked_x3")
+        square(1, recip1, whole)
+        after_x3 = keep.tile([P, 2 * N], F32, name="after_x3", tag="x3", align_bytes=64)
+        u2, step0 = after_x3[:, 0:N], after_x3[:, N : 2 * N]
+        recip2 = keep.tile([P, N], F32, name="recip2")
+        recip3 = keep.tile([P, N], F32, name="recip3")
+        mix(2, u2)
+        inverse_root(2, whole)
+        square(2, recip2, whole)
+        soft_sign(u0, recip0, step0, whole)
+        multiply(3, x3, "x_codes3")
+        late = keep.tile([P, 5 * N], F32, name="late", tag="x_grouped3", align_bytes=64)
+        y = late[:, 0 : 4 * N].rearrange("p (h t c) -> p h t c", h=2, t=PACK)
+        step1 = late[:, 4 * N : 5 * N]
+        decay(0, step0)
+        soft_sign(u1, recip1, step1, whole)
+        u3 = keep.tile([P, N], F32, name="u3")
+        mix(3, u3[:])
+        for h in range(2):
+            inverse_root(3, half[h])
+            square(3, recip3, half[h])
+        decay(1, step1)
+        step2 = mom_sb[3][:]
+        soft_sign(u2, recip2, step2, whole)
+        decay(2, step2)
+        step3 = old_sb[2][:]
+        words = out_1.rearrange("z l c r -> (z l) (c r)").bitcast(I32)
+        for h in range(2):
+            soft_sign(u3, recip3, step3, half[h])
+            nc.vector.scalar_tensor_tensor(y[:, h, 3, :], old_sb[3][:, half[h]], 0.3, step3[:, half[h]], ALU.mult, ALU.subtract)
+            nc.sync.dma_start(y_rows[:, 3, half[h]], y[:, h, 3, :])
+        nc.scalar.copy(y_grouped[0][:], y[:, 0].rearrange("p t n -> p n t"))
+        nc.vector.tensor_copy(y_grouped[1][:], y[:, 1].rearrange("p t n -> p n t"))
+        for h in range(2):
+            quantize(y_grouped[h], y_codes[:, half[h]], y_scales[:, half[h]], E4M3)
+            nc.sync.dma_start(words[:, half[h]], y_codes[:, half[h]].bitcast(I32))
+        scale_rows = out_2.rearrange("z q c -> (z q) c").bitcast(I32)
+        for q in range(4):
+            nc.scalar.dma_start(scale_rows[4 * q : 4 * q + 4, :], y_scales[32 * q : 32 * q + 4, :].bitcast(I32))

@@ -20,6 +20,7 @@ ACT = mybir.ActivationFunctionType
 P = 128
 PACK = 4
 HALF = N // 2
+QUARTER = N // 4
 
 
 def tile_moe_expert_soft_sign_step_pl_kernel(tc, xt, g, mom, old, offs, out_0, out_1, out_2):
@@ -38,8 +39,14 @@ def tile_moe_expert_soft_sign_step_pl_kernel(tc, xt, g, mom, old, offs, out_0, o
 
         g_win = [keep.tile([P, T], F32, name="g_win%d" % b) for b in range(4)]
         x_win = [keep.tile([P, T], F32, name="x_win%d" % t, tag="x%d" % t, align_bytes=64) for t in range(PACK)]
-        mom_sb = [keep.tile([P, N], F32, name="mom%d" % t) for t in range(PACK)]
-        old_sb = [keep.tile([P, N], F32, name="old%d" % t) for t in range(PACK)]
+        mom_01 = keep.tile([P, 2 * N], F32, name="mom_01")
+        mom_2 = keep.tile([P, N], F32, name="mom_2")
+        mom_3 = keep.tile([P, N], F32, name="mom_3")
+        mom_sb = [mom_01[:, 0:N], mom_01[:, N : 2 * N], mom_2[:], mom_3[:]]
+        old_0 = keep.tile([P, N], F32, name="old_0")
+        old_12 = keep.tile([P, 2 * N], F32, name="old_12")
+        old_3 = keep.tile([P, N], F32, name="old_3")
+        old_sb = [old_0[:], old_12[:, 0:N], old_12[:, N : 2 * N], old_3[:]]
 
         nc.sync.dma_start(g_win[0][:], g[0:P, :])
         nc.sync.dma_start(offsets[:], offs)
@@ -47,14 +54,13 @@ def tile_moe_expert_soft_sign_step_pl_kernel(tc, xt, g, mom, old, offs, out_0, o
             nc.sync.dma_start(g_win[b][:], g[b * P : (b + 1) * P, :])
         for t in range(3):
             nc.sync.dma_start(x_win[t][:], xt_rows[:, t, :])
-        for t in range(2):
-            nc.sync.dma_start(mom_sb[t][:], mom_rows[:, t, :])
+        nc.sync.dma_start(mom_01[:], mom_rows[:, 0:2, :].rearrange("p t n -> p (t n)"))
         nc.sync.dma_start(x_win[3][:], xt_rows[:, 3, :])
-        nc.sync.dma_start(mom_sb[2][:], mom_rows[:, 2, :])
-        nc.sync.dma_start(old_sb[0][:], old_rows[:, 0, :])
-        nc.sync.dma_start(mom_sb[3][:], mom_rows[:, 3, :])
-        for t in (3, 1, 2):
-            nc.sync.dma_start(old_sb[t][:], old_rows[:, t, :])
+        nc.sync.dma_start(mom_2[:], mom_rows[:, 2, :])
+        nc.sync.dma_start(old_0[:], old_rows[:, 0, :])
+        nc.sync.dma_start(mom_3[:], mom_rows[:, 3, :])
+        nc.sync.dma_start(old_3[:], old_rows[:, 3, :])
+        nc.sync.dma_start(old_12[:], old_rows[:, 1:3, :].rearrange("p t n -> p (t n)"))
 
         warm_in = keep.tile([P, 1], F32, name="warm_in")
         warm_out = keep.tile([P, 1], F32, name="warm_out")
@@ -101,7 +107,7 @@ def tile_moe_expert_soft_sign_step_pl_kernel(tc, xt, g, mom, old, offs, out_0, o
             )
 
         def mix(t, u):
-            nc.vector.scalar_tensor_tensor(u, w[t][:], 0.04 / 0.5, mom_sb[t][:], ALU.mult, ALU.add)
+            nc.vector.scalar_tensor_tensor(u, w[t][:], 0.04 / 0.5, mom_sb[t], ALU.mult, ALU.add)
             nc.scalar.activation(mag[t][:], u, ACT.Abs, scale=1.0 / N, accum_out=mean[t][:])
 
         def inverse_root(t, cols):
@@ -117,11 +123,12 @@ def tile_moe_expert_soft_sign_step_pl_kernel(tc, xt, g, mom, old, offs, out_0, o
             return ap.rearrange("p (h c) -> p h c", h=2)
 
         def decay(t, step):
-            nc.vector.scalar_tensor_tensor(y[:, :, t, :], halves(old_sb[t][:]), 0.3, halves(step), ALU.mult, ALU.subtract)
+            nc.vector.scalar_tensor_tensor(y[:, :, t, :], halves(old_sb[t]), 0.3, halves(step), ALU.mult, ALU.subtract)
             nc.sync.dma_start(halves(y_rows[:, t, :]), y[:, :, t, :])
 
         whole = slice(0, N)
         half = [slice(h * HALF, (h + 1) * HALF) for h in range(2)]
+        quarter = [slice(q * QUARTER, (q + 1) * QUARTER) for q in range(4)]
         for b in range(4):
             gather_and_turn(g_win[b], "g%d" % b, g_grouped[:, b * P : (b + 1) * P, :])
         x0 = turn_x(0)
@@ -142,12 +149,12 @@ def tile_moe_expert_soft_sign_step_pl_kernel(tc, xt, g, mom, old, offs, out_0, o
         inverse_root(1, whole)
         x3 = turn_x(3)
         recip1 = keep.tile([P, N], F32, name="recip1", tag="picked_x3")
-        square(1, recip1, whole)
         after_x3 = keep.tile([P, 2 * N], F32, name="after_x3", tag="x3", align_bytes=64)
         u2, step0 = after_x3[:, 0:N], after_x3[:, N : 2 * N]
         recip2 = keep.tile([P, N], F32, name="recip2")
         recip3 = keep.tile([P, N], F32, name="recip3")
         mix(2, u2)
+        square(1, recip1, whole)
         inverse_root(2, whole)
         square(2, recip2, whole)
         soft_sign(u0, recip0, step0, whole)
@@ -159,24 +166,40 @@ def tile_moe_expert_soft_sign_step_pl_kernel(tc, xt, g, mom, old, offs, out_0, o
         soft_sign(u1, recip1, step1, whole)
         u3 = keep.tile([P, N], F32, name="u3")
         mix(3, u3[:])
-        for h in range(2):
-            inverse_root(3, half[h])
-            square(3, recip3, half[h])
-        decay(1, step1)
-        step2 = mom_sb[3][:]
+        inverse_root(3, quarter[0])
+        for q in range(4):
+            if q < 3:
+                inverse_root(3, quarter[q + 1])
+            square(3, recip3, quarter[q])
+        step2 = keep.tile([P, N], F32, name="step2")
         soft_sign(u2, recip2, step2, whole)
-        decay(2, step2)
-        step3 = old_sb[2][:]
+        decay(1, step1)
+        decay(2, step2[:])
+        step3 = step1
+
+        def in_half(q):
+            return slice((q % 2) * QUARTER, (q % 2 + 1) * QUARTER)
+
+        def interleave(copy, q):
+            copy(
+                y_grouped[q // 2][:, in_half(q), :].rearrange("p (c i) t -> p c t i", i=4),
+                y[:, q // 2, :, in_half(q)].rearrange("p t (c i) -> p c t i", i=4),
+            )
+
+        soft_sign(u3, recip3, step3, quarter[0])
+        for q in range(4):
+            if q < 3:
+                soft_sign(u3, recip3, step3, quarter[q + 1])
+            nc.vector.scalar_tensor_tensor(y[:, q // 2, 3, in_half(q)], old_sb[3][:, quarter[q]], 0.3, step3[:, quarter[q]], ALU.mult, ALU.subtract)
+            if q % 2 == 1:
+                nc.sync.dma_start(y_rows[:, 3, half[q // 2]], y[:, q // 2, 3, :])
+        for q in range(4):
+            interleave(nc.scalar.copy if q < 2 else nc.vector.tensor_copy, q)
         words = out_1.rearrange("z l c r -> (z l) (c r)").bitcast(I32)
-        for h in range(2):
-            soft_sign(u3, recip3, step3, half[h])
-            nc.vector.scalar_tensor_tensor(y[:, h, 3, :], old_sb[3][:, half[h]], 0.3, step3[:, half[h]], ALU.mult, ALU.subtract)
-            nc.sync.dma_start(y_rows[:, 3, half[h]], y[:, h, 3, :])
-        nc.scalar.copy(y_grouped[0][:], y[:, 0].rearrange("p t n -> p n t"))
-        nc.vector.tensor_copy(y_grouped[1][:], y[:, 1].rearrange("p t n -> p n t"))
         for h in range(2):
             quantize(y_grouped[h], y_codes[:, half[h]], y_scales[:, half[h]], E4M3)
             nc.sync.dma_start(words[:, half[h]], y_codes[:, half[h]].bitcast(I32))
         scale_rows = out_2.rearrange("z q c -> (z q) c").bitcast(I32)
         for q in range(4):
-            nc.scalar.dma_start(scale_rows[4 * q : 4 * q + 4, :], y_scales[32 * q : 32 * q + 4, :].bitcast(I32))
+            queue = nc.sync if q == 0 else nc.scalar
+            queue.dma_start(scale_rows[4 * q : 4 * q + 4, :], y_scales[32 * q : 32 * q + 4, :].bitcast(I32))

@@ -37,15 +37,15 @@ def tile_moe_expert_soft_sign_step_pl_kernel(tc, xt, g, mom, old, offs, out_0, o
         old_rows = old.rearrange("(p t) n -> p t n", t=PACK)
         y_rows = out_0.rearrange("(p t) n -> p t n", t=PACK)
 
-        g_win = [keep.tile([P, T], F32, name="g_win%d" % b) for b in range(4)]
-        x_win = [keep.tile([P, T], F32, name="x_win%d" % t, tag="x%d" % t, align_bytes=64) for t in range(PACK)]
-        mom_01 = keep.tile([P, 2 * N], F32, name="mom_01")
-        mom_2 = keep.tile([P, N], F32, name="mom_2")
-        mom_3 = keep.tile([P, N], F32, name="mom_3")
+        g_win = [keep.tile([P, T], F32, name="g_win%d" % b, align_bytes=256) for b in range(4)]
+        x_win = [keep.tile([P, T], F32, name="x_win%d" % t, tag="x%d" % t, align_bytes=256) for t in range(PACK)]
+        mom_01 = keep.tile([P, 2 * N], F32, name="mom_01", align_bytes=256)
+        mom_2 = keep.tile([P, N], F32, name="mom_2", align_bytes=256)
+        mom_3 = keep.tile([P, N], F32, name="mom_3", align_bytes=256)
         mom_sb = [mom_01[:, 0:N], mom_01[:, N : 2 * N], mom_2[:], mom_3[:]]
-        old_0 = keep.tile([P, N], F32, name="old_0")
-        old_12 = keep.tile([P, 2 * N], F32, name="old_12")
-        old_3 = keep.tile([P, N], F32, name="old_3")
+        old_0 = keep.tile([P, N], F32, name="old_0", align_bytes=256)
+        old_12 = keep.tile([P, 2 * N], F32, name="old_12", align_bytes=256)
+        old_3 = keep.tile([P, N], F32, name="old_3", align_bytes=256)
         old_sb = [old_0[:], old_12[:, 0:N], old_12[:, N : 2 * N], old_3[:]]
 
         nc.sync.dma_start(g_win[0][:], g[0:P, :])
@@ -70,16 +70,16 @@ def tile_moe_expert_soft_sign_step_pl_kernel(tc, xt, g, mom, old, offs, out_0, o
         ident = keep.tile([P, P], F32, name="ident")
         make_identity(nc, ident[:])
 
-        g_grouped = keep.tile([P, N, PACK], BF16, name="g_grouped", align_bytes=64)
-        g_scales = keep.tile([P, N], U8, name="g_scales", align_bytes=64)
-        x_scales = [keep.tile([P, P], U8, name="x_scales%d" % t, align_bytes=64) for t in range(PACK)]
+        g_grouped = keep.tile([P, N, PACK], BF16, name="g_grouped", align_bytes=256)
+        g_scales = keep.tile([P, N], U8, name="g_scales", align_bytes=256)
+        x_scales = [keep.tile([P, P], U8, name="x_scales%d" % t, align_bytes=256) for t in range(PACK)]
         w = [sum_psum.tile([P, N], F32, name="w%d" % t) for t in range(PACK)]
         mag = [keep.tile([P, N], F32, name="mag%d" % t) for t in range(PACK)]
         mean = [keep.tile([P, 1], F32, name="mean%d" % t) for t in range(PACK)]
         root = [keep.tile([P, N], F32, name="root%d" % t) for t in range(PACK)]
-        y_grouped = [keep.tile([P, HALF, PACK], BF16, name="y_grouped%d" % h, align_bytes=64) for h in range(2)]
-        y_codes = keep.tile([P, N], U32, name="y_codes", align_bytes=64)
-        y_scales = keep.tile([P, N], U8, name="y_scales", align_bytes=64)
+        y_grouped = [keep.tile([P, HALF, PACK], BF16, name="y_grouped%d" % h, align_bytes=256) for h in range(2)]
+        y_codes = keep.tile([P, N], U32, name="y_codes", align_bytes=256)
+        y_scales = keep.tile([P, N], U8, name="y_scales", align_bytes=256)
 
         def gather_and_turn(window, name, grouped):
             picked = keep.tile([P, J], BF16, name="picked_" + name, tag="picked_" + name)
@@ -91,7 +91,7 @@ def tile_moe_expert_soft_sign_step_pl_kernel(tc, xt, g, mom, old, offs, out_0, o
             nc.scalar.copy(grouped.bitcast(F32), turned[:].rearrange("p e r -> p r e"))
 
         def turn_x(t):
-            grouped = keep.tile([P, P, PACK], BF16, name="x_grouped%d" % t, tag="x_grouped%d" % t, align_bytes=64)
+            grouped = keep.tile([P, P, PACK], BF16, name="x_grouped%d" % t, tag="x_grouped%d" % t, align_bytes=256)
             gather_and_turn(x_win[t], "x%d" % t, grouped[:])
             return grouped
 
@@ -99,7 +99,7 @@ def tile_moe_expert_soft_sign_step_pl_kernel(tc, xt, g, mom, old, offs, out_0, o
             nc.vector.quantize_mx(out=codes.bitcast(fmt), scales=scales, in_=grouped[:].rearrange("p c t -> p (c t)"))
 
         def multiply(t, grouped, tag):
-            codes = keep.tile([P, P], U32, name="x_codes%d" % t, tag=tag, align_bytes=64)
+            codes = keep.tile([P, P], U32, name="x_codes%d" % t, tag=tag, align_bytes=256)
             quantize(grouped, codes[:], x_scales[t][:], E4M3)
             nc.tensor.matmul_mx(
                 out=w[t][:], lhsT=codes[:].bitcast(E4M3), lhsT_scale=x_scales[t][:],
@@ -132,7 +132,7 @@ def tile_moe_expert_soft_sign_step_pl_kernel(tc, xt, g, mom, old, offs, out_0, o
         for b in range(4):
             gather_and_turn(g_win[b], "g%d" % b, g_grouped[:, b * P : (b + 1) * P, :])
         x0 = turn_x(0)
-        g_codes = keep.tile([P, N], U32, name="g_codes", tag="x0", align_bytes=64)
+        g_codes = keep.tile([P, N], U32, name="g_codes", tag="x0", align_bytes=256)
         quantize(g_grouped, g_codes[:], g_scales[:], E5M2)
         x1 = turn_x(1)
         multiply(0, x0, "x1")
@@ -149,7 +149,7 @@ def tile_moe_expert_soft_sign_step_pl_kernel(tc, xt, g, mom, old, offs, out_0, o
         inverse_root(1, whole)
         x3 = turn_x(3)
         recip1 = keep.tile([P, N], F32, name="recip1", tag="picked_x3")
-        after_x3 = keep.tile([P, 2 * N], F32, name="after_x3", tag="x3", align_bytes=64)
+        after_x3 = keep.tile([P, 2 * N], F32, name="after_x3", tag="x3", align_bytes=256)
         u2, step0 = after_x3[:, 0:N], after_x3[:, N : 2 * N]
         recip2 = keep.tile([P, N], F32, name="recip2")
         recip3 = keep.tile([P, N], F32, name="recip3")
@@ -159,7 +159,7 @@ def tile_moe_expert_soft_sign_step_pl_kernel(tc, xt, g, mom, old, offs, out_0, o
         square(2, recip2, whole)
         soft_sign(u0, recip0, step0, whole)
         multiply(3, x3, "x_codes3")
-        late = keep.tile([P, 5 * N], F32, name="late", tag="x_grouped3", align_bytes=64)
+        late = keep.tile([P, 5 * N], F32, name="late", tag="x_grouped3", align_bytes=256)
         y = late[:, 0 : 4 * N].rearrange("p (h t c) -> p h t c", h=2, t=PACK)
         step1 = late[:, 4 * N : 5 * N]
         decay(0, step0)

from contextlib import ExitStack

import concourse.mybir as mybir
from concourse.masks import make_identity

K, N, T, J = 512, 512, 2048, 512
FLOPS = 2 * K * N * J

F32 = mybir.dt.float32
BF16 = mybir.dt.bfloat16
I32 = mybir.dt.int32
U32 = mybir.dt.uint32
U16 = mybir.dt.uint16
U8 = mybir.dt.uint8
E4M3 = mybir.dt.float8_e4m3fn_x4
E5M2 = mybir.dt.float8_e5m2_x4
ALU = mybir.AluOpType
ACT = mybir.ActivationFunctionType

P = 128
PACK = 4
HALF = N // 2
QUARTER = N // 4


def tile_moe_expert_soft_sign_step_pl_kernel(tc, xt, g, mom, old, offs, out_0, out_1, out_2):
    nc = tc.nc
    with ExitStack() as ctx:
        keep = ctx.enter_context(tc.tile_pool(name="keep", bufs=1))
        turn_psum = ctx.enter_context(tc.psum_pool(name="turn_psum", bufs=4))
        sum_psum = ctx.enter_context(tc.psum_pool(name="sum_psum", bufs=1))

        offsets = keep.tile([P, J // 16], U16, name="offsets")

        xt_rows = xt.rearrange("(p t) c -> p t c", t=PACK)
        mom_rows = mom.rearrange("(p t) n -> p t n", t=PACK)
        old_rows = old.rearrange("(p t) n -> p t n", t=PACK)
        y_rows = out_0.rearrange("(p t) n -> p t n", t=PACK)

        g_win = [keep.tile([P, T], F32, name="g_win%d" % b, align_bytes=256) for b in range(4)]
        x_win = [keep.tile([P, T], F32, name="x_win%d" % t, tag="x%d" % t, align_bytes=256) for t in range(PACK)]
        mom_01 = keep.tile([P, 2 * N], F32, name="mom_01", align_bytes=256)
        mom_2 = keep.tile([P, N], F32, name="mom_2", align_bytes=256)
        mom_3 = keep.tile([P, N], F32, name="mom_3", align_bytes=256)
        mom_sb = [mom_01[:, 0:N], mom_01[:, N : 2 * N], mom_2[:], mom_3[:]]
        old_0 = keep.tile([P, N], F32, name="old_0", align_bytes=256)
        old_12 = keep.tile([P, 2 * N], F32, name="old_12", align_bytes=256)
        old_3 = keep.tile([P, N], F32, name="old_3", align_bytes=256)
        old_sb = [old_0[:], old_12[:, 0:N], old_12[:, N : 2 * N], old_3[:]]

        nc.sync.dma_start(g_win[0][:], g[0:P, :])
        nc.sync.dma_start(offsets[:], offs)
        for b in range(1, 4):
            nc.sync.dma_start(g_win[b][:], g[b * P : (b + 1) * P, :])
        for t in range(3):
            nc.sync.dma_start(x_win[t][:], xt_rows[:, t, :])
        nc.sync.dma_start(mom_01[:], mom_rows[:, 0:2, :].rearrange("p t n -> p (t n)"))
        nc.sync.dma_start(x_win[3][:], xt_rows[:, 3, :])
        nc.sync.dma_start(mom_2[:], mom_rows[:, 2, :])
        nc.sync.dma_start(old_0[:], old_rows[:, 0, :])
        nc.sync.dma_start(mom_3[:], mom_rows[:, 3, :])
        nc.sync.dma_start(old_3[:], old_rows[:, 3, :])
        nc.sync.dma_start(old_12[:], old_rows[:, 1:3, :].rearrange("p t n -> p (t n)"))

        warm_in = keep.tile([P, 1], F32, name="warm_in")
        warm_out = keep.tile([P, 1], F32, name="warm_out")
        nc.vector.memset(warm_in[:], 1.0)
        nc.scalar.activation(warm_out[:], warm_in[:], ACT.Abs_reciprocal_sqrt)

        ident = keep.tile([P, P], F32, name="ident")
        make_identity(nc, ident[:])

        g_grouped = keep.tile([P, N, PACK], BF16, name="g_grouped", align_bytes=256)
        g_scales = keep.tile([P, N], U8, name="g_scales", align_bytes=256)
        x_scales = [keep.tile([P, P], U8, name="x_scales%d" % t, align_bytes=256) for t in range(PACK)]
        w = [sum_psum.tile([P, N], F32, name="w%d" % t) for t in range(PACK)]
        mag = [keep.tile([P, N], F32, name="mag%d" % t) for t in range(PACK)]
        mean = [keep.tile([P, 1], F32, name="mean%d" % t) for t in range(PACK)]
        root = [keep.tile([P, N], F32, name="root%d" % t) for t in range(PACK)]
        y_grouped = [keep.tile([P, HALF, PACK], BF16, name="y_grouped%d" % h, align_bytes=256) for h in range(2)]
        y_codes = keep.tile([P, N], U32, name="y_codes", align_bytes=256)
        y_scales = keep.tile([P, N], U8, name="y_scales", align_bytes=256)

        def gather_and_turn(window, name, grouped):
            picked = keep.tile([P, J], BF16, name="picked_" + name, tag="picked_" + name)
            nc.vector.tensor_copy(picked[:], window[:].indirect(offsets[:]))
            words = picked[:].bitcast(F32)
            turned = turn_psum.tile([P, 2, P], F32, name="turned")
            for e in range(2):
                nc.tensor.transpose(turned[:, e, :], words[:, e::2], ident[:])
            nc.scalar.copy(grouped.bitcast(F32), turned[:].rearrange("p e r -> p r e"))

        def turn_x(t):
            grouped = keep.tile([P, P, PACK], BF16, name="x_grouped%d" % t, tag="x_grouped%d" % t, align_bytes=256)
            gather_and_turn(x_win[t], "x%d" % t, grouped[:])
            return grouped

        def quantize(grouped, codes, scales, fmt):
            nc.vector.quantize_mx(out=codes.bitcast(fmt), scales=scales, in_=grouped[:].rearrange("p c t -> p (c t)"))

        def multiply(t, grouped, tag):
            codes = keep.tile([P, P], U32, name="x_codes%d" % t, tag=tag, align_bytes=256)
            quantize(grouped, codes[:], x_scales[t][:], E4M3)
            nc.tensor.matmul_mx(
                out=w[t][:], lhsT=codes[:].bitcast(E4M3), lhsT_scale=x_scales[t][:],
                rhs=g_codes[:].bitcast(E5M2), rhs_scale=g_scales[:], start=True, stop=True,
            )

        def mix(t, u):
            nc.vector.scalar_tensor_tensor(u, w[t][:], 0.04 / 0.5, mom_sb[t], ALU.mult, ALU.add)
            nc.scalar.activation(mag[t][:], u, ACT.Abs, scale=1.0 / N, accum_out=mean[t][:])

        def inverse_root(t, cols):
            nc.scalar.activation(root[t][:, cols], mag[t][:, cols], ACT.Abs_reciprocal_sqrt, bias=mean[t][:], scale=float(N))

        def square(t, recip, cols):
            nc.scalar.activation(recip[:, cols], root[t][:, cols], ACT.Square)

        def soft_sign(u, recip, step, cols):
            nc.vector.tensor_tensor(step[:, cols], u[:, cols], recip[:, cols], ALU.mult)

        def halves(ap):
            return ap.rearrange("p (h c) -> p h c", h=2)

        def decay(t, step):
            nc.vector.scalar_tensor_tensor(y[:, :, t, :], halves(old_sb[t]), 0.3, halves(step), ALU.mult, ALU.subtract)
            nc.sync.dma_start(halves(y_rows[:, t, :]), y[:, :, t, :])

        whole = slice(0, N)
        half = [slice(h * HALF, (h + 1) * HALF) for h in range(2)]
        quarter = [slice(q * QUARTER, (q + 1) * QUARTER) for q in range(4)]
        for b in range(4):
            gather_and_turn(g_win[b], "g%d" % b, g_grouped[:, b * P : (b + 1) * P, :])
        x0 = turn_x(0)
        g_codes = keep.tile([P, N], U32, name="g_codes", tag="x0", align_bytes=256)
        quantize(g_grouped, g_codes[:], g_scales[:], E5M2)
        x1 = turn_x(1)
        multiply(0, x0, "x1")
        x2 = turn_x(2)
        multiply(1, x1, "x2")
        u0 = keep.tile([P, N], F32, name="u0")
        u1 = keep.tile([P, N], F32, name="u1")
        recip0 = keep.tile([P, N], F32, name="recip0")
        mix(0, u0[:])
        inverse_root(0, whole)
        square(0, recip0, whole)
        multiply(2, x2, "x_codes2")
        mix(1, u1[:])
        inverse_root(1, whole)
        x3 = turn_x(3)
        recip1 = keep.tile([P, N], F32, name="recip1", tag="picked_x3")
        after_x3 = keep.tile([P, 2 * N], F32, name="after_x3", tag="x3", align_bytes=256)
        u2, step0 = after_x3[:, 0:N], after_x3[:, N : 2 * N]
        recip2 = keep.tile([P, N], F32, name="recip2")
        recip3 = keep.tile([P, N], F32, name="recip3")
        mix(2, u2)
        square(1, recip1, whole)
        inverse_root(2, whole)
        square(2, recip2, whole)
        soft_sign(u0, recip0, step0, whole)
        multiply(3, x3, "x_codes3")
        late = keep.tile([P, 5 * N], F32, name="late", tag="x_grouped3", align_bytes=256)
        y = late[:, 0 : 4 * N].rearrange("p (h t c) -> p h t c", h=2, t=PACK)
        step1 = late[:, 4 * N : 5 * N]
        decay(0, step0)
        soft_sign(u1, recip1, step1, whole)
        u3 = keep.tile([P, N], F32, name="u3")
        mix(3, u3[:])
        inverse_root(3, quarter[0])
        for q in range(4):
            if q < 3:
                inverse_root(3, quarter[q + 1])
            square(3, recip3, quarter[q])
        step2 = keep.tile([P, N], F32, name="step2")
        soft_sign(u2, recip2, step2, whole)
        decay(1, step1)
        decay(2, step2[:])
        step3 = step1

        def in_half(q):
            return slice((q % 2) * QUARTER, (q % 2 + 1) * QUARTER)

        def interleave(copy, q):
            copy(
                y_grouped[q // 2][:, in_half(q), :].rearrange("p (c i) t -> p c t i", i=4),
                y[:, q // 2, :, in_half(q)].rearrange("p t (c i) -> p c t i", i=4),
            )

        soft_sign(u3, recip3, step3, quarter[0])
        for q in range(4):
            if q < 3:
                soft_sign(u3, recip3, step3, quarter[q + 1])
            nc.vector.scalar_tensor_tensor(y[:, q // 2, 3, in_half(q)], old_sb[3][:, quarter[q]], 0.3, step3[:, quarter[q]], ALU.mult, ALU.subtract)
            if q % 2 == 1:
                nc.sync.dma_start(y_rows[:, 3, half[q // 2]], y[:, q // 2, 3, :])
        for q in range(4):
            interleave(nc.scalar.copy if q < 2 else nc.vector.tensor_copy, q)
        words = out_1.rearrange("z l c r -> (z l) (c r)").bitcast(I32)
        for h in range(2):
            quantize(y_grouped[h], y_codes[:, half[h]], y_scales[:, half[h]], E4M3)
            nc.sync.dma_start(words[:, half[h]], y_codes[:, half[h]].bitcast(I32))
        scale_rows = out_2.rearrange("z q c -> (z q) c").bitcast(I32)
        for q in range(4):
            queue = nc.sync if q == 0 else nc.scalar
            queue.dma_start(scale_rows[4 * q : 4 * q + 4, :], y_scales[32 * q : 32 * q + 4, :].bitcast(I32))
